import numpy as np
import ml_dtypes


def mxq(x, axis, fmt="e4m3"):
    dtype, down = {"e4m3": (ml_dtypes.float8_e4m3fn, 7), "e5m2": (ml_dtypes.float8_e5m2, 14)}[fmt]
    v = np.moveaxis(np.asarray(x, np.float32).astype(ml_dtypes.bfloat16).astype(np.float64), axis, -1)
    blocks = v.reshape(v.shape[:-1] + (-1, 32))
    amax = np.abs(blocks).max(-1, keepdims=True)
    byte = np.maximum(np.where(amax > 0, np.frexp(amax)[1] - 1 + 127, 0) - down, 1)
    scale = np.exp2(byte - 127.0)
    codes = (blocks / scale).astype(np.float32).astype(dtype).astype(np.float64)
    return np.moveaxis((codes * scale).reshape(v.shape), -1, axis)


WIDE = False


def mx_kscale(k):
    if not WIDE:
        return np.ones(k)
    levels = np.array([10, -10, 5, -5, 0])
    if k % 512:
        return np.exp2(np.random.permutation(np.resize(levels, k // 32))).repeat(32)
    a = np.empty((k // 512, 16))
    for p in range(k // 512):
        a[p, :8] = np.random.permutation(np.resize(levels, 8))
        for g in range(8):
            far = levels[np.abs(levels - a[p, g]) >= 10]
            a[p, g + 8] = far[np.random.randint(len(far))]
    return np.exp2(a.ravel()).repeat(32)


def f64(x):
    return np.asarray(x).astype(np.float64)


def striped(idx):
    return np.tile(idx.reshape(-1, 16).T, (8, 1)).astype(np.uint16)


def unstriped(offs):
    return offs[:16].T.reshape(-1).astype(np.int64)


def pack_weight(w):
    k, n = w.shape
    w = f64(np.asarray(w, np.float32).astype(ml_dtypes.bfloat16)).reshape(k // 32, 32, n)
    amax = np.abs(w).max(1)
    byte = np.clip(np.where(amax > 0, np.frexp(amax)[1] - 1 + 127 - 7, 1), 1, 254)
    scaled = (w * np.exp2(127.0 - byte)[:, None, :]).reshape(k, n).astype(np.float32)
    words = np.ascontiguousarray(scaled.reshape(k // 512, 128, 4, n).transpose(0, 1, 3, 2)).astype(ml_dtypes.float8_e4m3fn).view(np.uint8)
    return words, np.ascontiguousarray(byte.astype(np.uint8).reshape(k // 512, 16, n))


def unpack_weight(words, scales):
    g, p, n, _ = words.shape
    vals = np.ascontiguousarray(words).view(ml_dtypes.float8_e4m3fn).astype(np.float64) * np.repeat(np.exp2(scales.astype(np.float64) - 127.0), 8, axis=1)[..., None]
    return vals.transpose(0, 1, 3, 2).reshape(g * 512, n)


K, T, S, V = 512, 1024, 512, 512
P = 2 ** 7


def setup_inputs():
    n = np.random.standard_normal
    s = mx_kscale(K)[:, None]
    packed_xT = pack_weight(n((K, T)) * s)
    return {
        "x_words": packed_xT[0],
        "x_scales": packed_xT[1],
        "hT": (n((K, V)) / np.sqrt(K) / s).astype(np.float32),
        "ratio": (np.random.uniform(0.0, 2.0, (V, S)) ** 2).astype(np.float32),
        "rate": (np.tile(np.random.uniform(0.3, 1.5, S), (P, 1))).astype(np.float32),
        "step": (np.tile(np.random.uniform(0.05, 0.4, S), (P, 1))).astype(np.float32),
        "cap": (np.tile(np.random.uniform(0.2, 0.6, S), (P, 1))).astype(np.float32),
        "offs": striped(np.random.permutation(T)[:S]),
    }


def reference(x_words, x_scales, hT, ratio, rate, step, cap, offs):
    hTq = mxq(f64(hT), 0, "e4m3")
    xq = unpack_weight(x_words, x_scales)[:, unstriped(offs)]
    y = 0.7 * (hTq.T @ xq)
    sc = np.exp(y)
    lea = np.minimum((f64(step)[:1] * f64(rate)[:1]) * sc, f64(cap)[:1])
    tot = lea.sum(axis=1, keepdims=True)
    return 100.0 * (lea / (tot + 5.0) + 0.01 * (lea * f64(ratio)))

@@ -1,0 +1,148 @@
+from contextlib import ExitStack
+
+import concourse.mybir as mybir
+from concourse.masks import make_identity
+
+K, T, S, V = 512, 1024, 512, 512
+FLOPS = 2 * K * S * V
+
+F32 = mybir.dt.float32
+BF16 = mybir.dt.bfloat16
+I32 = mybir.dt.int32
+U32 = mybir.dt.uint32
+U16 = mybir.dt.uint16
+U8 = mybir.dt.uint8
+FP8X4 = mybir.dt.float8_e4m3fn_x4
+ACT = mybir.ActivationFunctionType
+ALU = mybir.AluOpType
+
+P = 128
+PACK = 4
+NB = S // P
+HALF = V // 2
+
+
+def tile_picked_ysedd_leave_p_kernel(tc, x_words, x_scales, hT, ratio, rate, step, cap, offs, out):
+    nc = tc.nc
+    with ExitStack() as ctx:
+        sb = ctx.enter_context(tc.tile_pool(name="sb", bufs=1))
+        ps = ctx.enter_context(tc.psum_pool(name="ps", bufs=1))
+
+        offsets = sb.tile([P, S // 16], U16, name="offsets")
+        nc.sync.dma_start(offsets[:], offs)
+
+        scale_table = sb.tile([P, T], U8, name="scale_table", align_bytes=64)
+        nc.gpsimd.memset(scale_table[:].bitcast(I32), 0)
+        rows = sb.tile([P, P], F32, name="rows")
+        nc.gpsimd.memset(rows[:], 0.0)
+
+        h_view = hT.rearrange("(p j) t -> p j t", j=PACK)
+        h_raw = [sb.tile([P, PACK, HALF], F32, name="h_raw%d" % u, tag="stage", bufs=2) for u in range(2)]
+        nc.sync.dma_start(h_raw[0][:], h_view[:, :, 0:HALF])
+        for q in range(4):
+            nc.scalar.dma_start(
+                scale_table[32 * q : 32 * q + 4, :].bitcast(I32), x_scales[0, 4 * q : 4 * q + 4, :].bitcast(I32)
+            )
+        warm = sb.tile([P, 1], F32, name="warm")
+        nc.scalar.activation(warm[:], rows[:, 0:1], ACT.Exp)
+        word_table = sb.tile([P, T], I32, name="word_table", align_bytes=64)
+        nc.sync.dma_start(word_table[:], x_words[0].rearrange("p n t -> p (n t)").bitcast(I32))
+        nc.sync.dma_start(h_raw[1][:], h_view[:, :, HALF:V])
+        ident = sb.tile([P, P], F32, name="ident")
+        make_identity(nc, ident[:])
+        for i, vec in enumerate((rate, step, cap)):
+            nc.gpsimd.dma_start(rows[NB * i : NB * (i + 1), :], vec[0].rearrange("(c p) -> c p", p=P))
+
+        cols_ps = ps.tile([P, S], F32, name="cols_ps", tag="turned", bufs=4)
+        nc.tensor.transpose(cols_ps[:, 0:P], rows[:], ident[:])
+        cols = sb.tile([P, 3 * NB], F32, name="cols")
+        nc.scalar.copy(cols[:], cols_ps[:, 0 : 3 * NB])
+        reach = sb.tile([P, NB], F32, name="reach")
+        nc.vector.tensor_tensor(reach[:], cols[:, NB : 2 * NB], cols[:, 0:NB], ALU.mult)
+
+        x_scale = sb.tile([P, S], U8, name="x_scale", align_bytes=64)
+        nc.vector.tensor_copy(x_scale[:], scale_table[:].indirect(offsets[:]))
+        x_codes = [sb.tile([P, P], U32, name="x_codes%d" % c, align_bytes=64) for c in range(NB)]
+
+        def gather(c):
+            nc.vector.tensor_copy(x_codes[c][:], word_table[:].bitcast(U32).indirect(offsets[:, 8 * c : 8 * (c + 1)]))
+
+        h_codes = [sb.tile([P, HALF], U32, name="h_codes%d" % u, align_bytes=64) for u in range(2)]
+        h_scale = [sb.tile([P, HALF], U8, name="h_scale%d" % u, align_bytes=64) for u in range(2)]
+
+        def weave(b, copy):
+            u, w = divmod(b, 2)
+            g = sb.tile([P, P, PACK], BF16, name="grouped%d" % b, align_bytes=64)
+            copy(
+                g[:].rearrange("p (c i) j -> p c j i", i=4),
+                h_raw[u][:, :, w * P : (w + 1) * P].rearrange("p j (c i) -> p c j i", i=4),
+            )
+            return g
+
+        def quantize(b, g):
+            u, w = divmod(b, 2)
+            nc.vector.quantize_mx(
+                out=h_codes[u][:, w * P : (w + 1) * P].bitcast(FP8X4),
+                scales=h_scale[u][:, w * P : (w + 1) * P],
+                in_=g[:].rearrange("p t j -> p (t j)"),
+            )
+
+        g0 = weave(0, nc.scalar.copy)
+        g1 = weave(1, nc.vector.tensor_copy)
+        quantize(0, g0)
+        quantize(1, g1)
+        for c in range(NB):
+            gather(c)
+        g2 = weave(2, nc.scalar.copy)
+        g3 = weave(3, nc.vector.tensor_copy)
+        quantize(2, g2)
+        quantize(3, g3)
+
+        ratios = [sb.tile([P, 2, S], F32, name="ratio%d" % u, tag="stage", bufs=2) for u in range(2)]
+        for u in range(2):
+            nc.sync.dma_start(ratios[u][:], ratio[u * HALF : (u + 1) * HALF, :].rearrange("(w p) j -> p w j", p=P))
+
+        lea = {}
+
+        def product(u):
+            for pair in range(NB // 2):
+                y = ps.tile([P, 2, HALF], F32, name="y%d%d" % (u, pair))
+                for e in range(2):
+                    c = 2 * pair + e
+                    nc.tensor.matmul_mx(
+                        out=y[:, e, :],
+                        lhsT=x_codes[c][:].bitcast(FP8X4),
+                        lhsT_scale=x_scale[:, c * P : (c + 1) * P],
+                        rhs=h_codes[u][:].bitcast(FP8X4),
+                        rhs_scale=h_scale[u][:],
+                        start=True,
+                        stop=True,
+                    )
+                sc = sb.tile([P, 2, HALF], F32, name="sc%d%d" % (u, pair))
+                nc.scalar.activation(sc[:], y[:], ACT.Exp, scale=0.7)
+                for e in range(2):
+                    c = 2 * pair + e
+                    capped = sb.tile([P, HALF], F32, name="lea%d%d" % (u, c))
+                    nc.vector.tensor_scalar(
+                        capped[:], sc[:, e, :], reach[:, c : c + 1], cols[:, 2 * NB + c : 2 * NB + c + 1], ALU.mult, ALU.min
+                    )
+                    lea[(u, c)] = capped
+
+        def finish(b):
+            u, w = divmod(b, 2)
+            turned = ps.tile([P, S], F32, name="turned%d" % b, tag="turned", bufs=4)
+            for c in range(NB):
+                nc.tensor.transpose(turned[:, c * P : (c + 1) * P], lea[(u, c)][:, w * P : (w + 1) * P], ident[:])
+            terms = sb.tile([P, S], BF16, name="terms%d" % b)
+            den = sb.tile([P, 1], F32, name="den%d" % b)
+            nc.scalar.activation(terms[:], turned[:], ACT.Copy, scale=0.01, bias=0.05 / S, accum_out=den[:])
+            inv = sb.tile([P, 1], F32, name="inv%d" % b)
+            nc.vector.reciprocal(inv[:], den[:])
+            res = sb.tile([P, S], F32, name="res%d" % b)
+            nc.vector.scalar_tensor_tensor(res[:], ratios[u][:, w, :], inv[:], turned[:], ALU.add, ALU.mult)
+            nc.sync.dma_start(out[b * P : (b + 1) * P, :], res[:])
+
+        product(0)
+        product(1)
+        for b in range(V // P):
+            finish(b)

@@ -26,85 +26,73 @@ def tile_picked_ysedd_leave_p_kernel(tc, x_words, x_scales, hT, ratio, rate, ste
     nc = tc.nc
     with ExitStack() as ctx:
         sb = ctx.enter_context(tc.tile_pool(name="sb", bufs=1))
+        shared = ctx.enter_context(tc.tile_pool(name="shared", bufs=1))
         ps = ctx.enter_context(tc.psum_pool(name="ps", bufs=1))
 
         offsets = sb.tile([P, S // 16], U16, name="offsets")
         nc.sync.dma_start(offsets[:], offs)
 
-        scale_table = sb.tile([P, T], U8, name="scale_table", align_bytes=64)
-        nc.gpsimd.memset(scale_table[:].bitcast(I32), 0)
-        rows = sb.tile([P, P], F32, name="rows")
-        nc.gpsimd.memset(rows[:], 0.0)
-
         h_view = hT.rearrange("(p j) t -> p j t", j=PACK)
-        h_raw = [sb.tile([P, PACK, HALF], F32, name="h_raw%d" % u, tag="stage", bufs=2) for u in range(2)]
+        h_raw = [sb.tile([P, PACK, HALF], F32, name="h_raw%d" % u, tag="h_raw%d" % u) for u in range(2)]
         nc.sync.dma_start(h_raw[0][:], h_view[:, :, 0:HALF])
+        scale_table = sb.tile([P, T], U8, name="scale_table", tag="bytes", align_bytes=64)
+        nc.gpsimd.memset(scale_table[:].bitcast(I32), 0)
         for q in range(4):
-            nc.scalar.dma_start(
+            nc.sync.dma_start(
                 scale_table[32 * q : 32 * q + 4, :].bitcast(I32), x_scales[0, 4 * q : 4 * q + 4, :].bitcast(I32)
             )
-        warm = sb.tile([P, 1], F32, name="warm")
-        nc.scalar.activation(warm[:], rows[:, 0:1], ACT.Exp)
         word_table = sb.tile([P, T], I32, name="word_table", align_bytes=64)
         nc.sync.dma_start(word_table[:], x_words[0].rearrange("p n t -> p (n t)").bitcast(I32))
         nc.sync.dma_start(h_raw[1][:], h_view[:, :, HALF:V])
+        rate_col = sb.tile([P, NB], F32, name="rate_col")
+        step_col = sb.tile([P, NB], F32, name="step_col")
+        cap_col = sb.tile([P, NB], F32, name="cap_col")
+        with nc.allow_non_contiguous_dma(reason="one value a partition and block"):
+            for col, vec in ((rate_col, rate), (step_col, step), (cap_col, cap)):
+                nc.sync.dma_start(col[:], vec[0].rearrange("(c p) -> p c", p=P))
+
         ident = sb.tile([P, P], F32, name="ident")
         make_identity(nc, ident[:])
-        for i, vec in enumerate((rate, step, cap)):
-            nc.gpsimd.dma_start(rows[NB * i : NB * (i + 1), :], vec[0].rearrange("(c p) -> c p", p=P))
-
-        cols_ps = ps.tile([P, S], F32, name="cols_ps", tag="turned", bufs=4)
-        nc.tensor.transpose(cols_ps[:, 0:P], rows[:], ident[:])
-        cols = sb.tile([P, 3 * NB], F32, name="cols")
-        nc.scalar.copy(cols[:], cols_ps[:, 0 : 3 * NB])
-        reach = sb.tile([P, NB], F32, name="reach")
-        nc.vector.tensor_tensor(reach[:], cols[:, NB : 2 * NB], cols[:, 0:NB], ALU.mult)
+        warm = sb.tile([P, 1], F32, name="warm")
+        nc.scalar.activation(warm[:], ident[:, 0:1], ACT.Exp)
 
         x_scale = sb.tile([P, S], U8, name="x_scale", align_bytes=64)
         nc.vector.tensor_copy(x_scale[:], scale_table[:].indirect(offsets[:]))
-        x_codes = [sb.tile([P, P], U32, name="x_codes%d" % c, align_bytes=64) for c in range(NB)]
-
-        def gather(c):
-            nc.vector.tensor_copy(x_codes[c][:], word_table[:].bitcast(U32).indirect(offsets[:, 8 * c : 8 * (c + 1)]))
 
         h_codes = [sb.tile([P, HALF], U32, name="h_codes%d" % u, align_bytes=64) for u in range(2)]
-        h_scale = [sb.tile([P, HALF], U8, name="h_scale%d" % u, align_bytes=64) for u in range(2)]
+        h_scale = [
+            sb.tile([P, HALF], U8, name="h_scale0", tag="bytes", align_bytes=64),
+            sb.tile([P, HALF], U8, name="h_scale1", align_bytes=64),
+        ]
 
-        def weave(b, copy):
-            u, w = divmod(b, 2)
-            g = sb.tile([P, P, PACK], BF16, name="grouped%d" % b, align_bytes=64)
-            copy(
+        def quantize(u):
+            g = shared.tile([P, HALF, PACK], BF16, name="grouped%d" % u, align_bytes=64, offset=u * HALF * PACK * 2)
+            nc.scalar.copy(
                 g[:].rearrange("p (c i) j -> p c j i", i=4),
-                h_raw[u][:, :, w * P : (w + 1) * P].rearrange("p j (c i) -> p c j i", i=4),
+                h_raw[u][:].rearrange("p j (c i) -> p c j i", i=4),
             )
-            return g
-
-        def quantize(b, g):
-            u, w = divmod(b, 2)
             nc.vector.quantize_mx(
-                out=h_codes[u][:, w * P : (w + 1) * P].bitcast(FP8X4),
-                scales=h_scale[u][:, w * P : (w + 1) * P],
-                in_=g[:].rearrange("p t j -> p (t j)"),
+                out=h_codes[u][:].bitcast(FP8X4), scales=h_scale[u][:], in_=g[:].rearrange("p t j -> p (t j)")
             )
 
-        g0 = weave(0, nc.scalar.copy)
-        g1 = weave(1, nc.vector.tensor_copy)
-        quantize(0, g0)
-        quantize(1, g1)
+        quantize(0)
+        x_codes = [shared.tile([P, P], U32, name="x_codes%d" % c, align_bytes=64, offset=c * P * 4) for c in range(NB)]
         for c in range(NB):
-            gather(c)
-        g2 = weave(2, nc.scalar.copy)
-        g3 = weave(3, nc.vector.tensor_copy)
-        quantize(2, g2)
-        quantize(3, g3)
+            nc.vector.tensor_copy(
+                x_codes[c][:], word_table[:].bitcast(U32).indirect(offsets[:, 8 * c : 8 * (c + 1)])
+            )
+        quantize(1)
+        reach = sb.tile([P, NB], F32, name="reach")
+        nc.vector.tensor_tensor(reach[:], step_col[:], rate_col[:], ALU.mult)
 
-        ratios = [sb.tile([P, 2, S], F32, name="ratio%d" % u, tag="stage", bufs=2) for u in range(2)]
+        ratios = [sb.tile([P, 2, S], F32, name="ratio%d" % u) for u in range(2)]
         for u in range(2):
             nc.sync.dma_start(ratios[u][:], ratio[u * HALF : (u + 1) * HALF, :].rearrange("(w p) j -> p w j", p=P))
 
         lea = {}
 
         def product(u):
+            sc = sb.tile([P, NB, HALF], F32, name="sc%d" % u, tag="h_raw%d" % (1 - u))
             for pair in range(NB // 2):
                 y = ps.tile([P, 2, HALF], F32, name="y%d%d" % (u, pair))
                 for e in range(2):
@@ -118,31 +106,44 @@ def tile_picked_ysedd_leave_p_kernel(tc, x_words, x_scales, hT, ratio, rate, ste
                         start=True,
                         stop=True,
                     )
-                sc = sb.tile([P, 2, HALF], F32, name="sc%d%d" % (u, pair))
-                nc.scalar.activation(sc[:], y[:], ACT.Exp, scale=0.7)
+                nc.scalar.activation(sc[:, 2 * pair : 2 * pair + 2, :], y[:], ACT.Exp, scale=0.7)
                 for e in range(2):
                     c = 2 * pair + e
                     capped = sb.tile([P, HALF], F32, name="lea%d%d" % (u, c))
                     nc.vector.tensor_scalar(
-                        capped[:], sc[:, e, :], reach[:, c : c + 1], cols[:, 2 * NB + c : 2 * NB + c + 1], ALU.mult, ALU.min
+                        capped[:], sc[:, c, :], reach[:, c : c + 1], cap_col[:, c : c + 1], ALU.mult, ALU.min
                     )
                     lea[(u, c)] = capped
 
-        def finish(b):
+        turned = {}
+        inv = {}
+
+        def normaliser(b):
             u, w = divmod(b, 2)
-            turned = ps.tile([P, S], F32, name="turned%d" % b, tag="turned", bufs=4)
+            turned[b] = ps.tile([P, S], F32, name="turned%d" % b)
             for c in range(NB):
-                nc.tensor.transpose(turned[:, c * P : (c + 1) * P], lea[(u, c)][:, w * P : (w + 1) * P], ident[:])
+                nc.tensor.transpose(turned[b][:, c * P : (c + 1) * P], lea[(u, c)][:, w * P : (w + 1) * P], ident[:])
             terms = sb.tile([P, S], BF16, name="terms%d" % b)
             den = sb.tile([P, 1], F32, name="den%d" % b)
-            nc.scalar.activation(terms[:], turned[:], ACT.Copy, scale=0.01, bias=0.05 / S, accum_out=den[:])
-            inv = sb.tile([P, 1], F32, name="inv%d" % b)
-            nc.vector.reciprocal(inv[:], den[:])
+            nc.scalar.activation(terms[:], turned[b][:], ACT.Copy, scale=0.01, bias=0.05 / S, accum_out=den[:])
+            inv[b] = sb.tile([P, 1], F32, name="inv%d" % b)
+            nc.vector.reciprocal(inv[b][:], den[:])
+
+        def finish(b):
+            u, w = divmod(b, 2)
             res = sb.tile([P, S], F32, name="res%d" % b)
-            nc.vector.scalar_tensor_tensor(res[:], ratios[u][:, w, :], inv[:], turned[:], ALU.add, ALU.mult)
-            nc.sync.dma_start(out[b * P : (b + 1) * P, :], res[:])
+            for cols in (slice(0, S // 2), slice(S // 2, S)):
+                nc.vector.scalar_tensor_tensor(
+                    res[:, cols], ratios[u][:, w, cols], inv[b][:], turned[b][:, cols], ALU.add, ALU.mult
+                )
+                if b == V // P - 1:
+                    nc.sync.dma_start(out[b * P : (b + 1) * P, cols], res[:, cols])
+            if b < V // P - 1:
+                nc.sync.dma_start(out[b * P : (b + 1) * P, :], res[:])
 
         product(0)
         product(1)
+        for b in range(V // P):
+            normaliser(b)
         for b in range(V // P):
             finish(b)

@@ -26,17 +26,15 @@ def tile_picked_ysedd_leave_p_kernel(tc, x_words, x_scales, hT, ratio, rate, ste
     nc = tc.nc
     with ExitStack() as ctx:
         sb = ctx.enter_context(tc.tile_pool(name="sb", bufs=1))
-        shared = ctx.enter_context(tc.tile_pool(name="shared", bufs=1))
         ps = ctx.enter_context(tc.psum_pool(name="ps", bufs=1))
 
+        h_view = hT.rearrange("(p j) t -> p j t", j=PACK)
+        h_raw = [sb.tile([P, PACK, HALF], F32, name="h_raw%d" % u) for u in range(2)]
+        nc.sync.dma_start(h_raw[0][:], h_view[:, :, 0:HALF])
         offsets = sb.tile([P, S // 16], U16, name="offsets")
         nc.sync.dma_start(offsets[:], offs)
-
-        h_view = hT.rearrange("(p j) t -> p j t", j=PACK)
-        h_raw = [sb.tile([P, PACK, HALF], F32, name="h_raw%d" % u, tag="h_raw%d" % u) for u in range(2)]
-        nc.sync.dma_start(h_raw[0][:], h_view[:, :, 0:HALF])
-        scale_table = sb.tile([P, T], U8, name="scale_table", tag="bytes", align_bytes=64)
-        nc.gpsimd.memset(scale_table[:].bitcast(I32), 0)
+        scale_table = sb.tile([P, T], U8, name="scale_table", tag="scale_table", align_bytes=64)
+        nc.vector.memset(scale_table[:].bitcast(I32), 0)
         for q in range(4):
             nc.sync.dma_start(
                 scale_table[32 * q : 32 * q + 4, :].bitcast(I32), x_scales[0, 4 * q : 4 * q + 4, :].bitcast(I32)
@@ -44,12 +42,15 @@ def tile_picked_ysedd_leave_p_kernel(tc, x_words, x_scales, hT, ratio, rate, ste
         word_table = sb.tile([P, T], I32, name="word_table", align_bytes=64)
         nc.sync.dma_start(word_table[:], x_words[0].rearrange("p n t -> p (n t)").bitcast(I32))
         nc.sync.dma_start(h_raw[1][:], h_view[:, :, HALF:V])
-        rate_col = sb.tile([P, NB], F32, name="rate_col")
-        step_col = sb.tile([P, NB], F32, name="step_col")
-        cap_col = sb.tile([P, NB], F32, name="cap_col")
-        with nc.allow_non_contiguous_dma(reason="one value a partition and block"):
-            for col, vec in ((rate_col, rate), (step_col, step), (cap_col, cap)):
-                nc.sync.dma_start(col[:], vec[0].rearrange("(c p) -> p c", p=P))
+        rows = sb.tile([P, P], F32, name="rows", align_bytes=64)
+        nc.gpsimd.memset(rows[:], 0.0)
+        for r, vec in enumerate((rate, step, cap)):
+            nc.sync.dma_start(
+                rows[r:P:32, :].rearrange("q (c i) -> q c i", c=NB), vec[0].rearrange("(c q i) -> q c i", c=NB, q=4)
+            )
+        ratios = [sb.tile([P, 2, S], F32, name="ratio%d" % u) for u in range(2)]
+        for u in range(2):
+            nc.sync.dma_start(ratios[u][:], ratio[u * HALF : (u + 1) * HALF, :].rearrange("(w p) j -> p w j", p=P))
 
         ident = sb.tile([P, P], F32, name="ident")
         make_identity(nc, ident[:])
@@ -59,70 +60,72 @@ def tile_picked_ysedd_leave_p_kernel(tc, x_words, x_scales, hT, ratio, rate, ste
         x_scale = sb.tile([P, S], U8, name="x_scale", align_bytes=64)
         nc.vector.tensor_copy(x_scale[:], scale_table[:].indirect(offsets[:]))
 
-        h_codes = [sb.tile([P, HALF], U32, name="h_codes%d" % u, align_bytes=64) for u in range(2)]
-        h_scale = [
-            sb.tile([P, HALF], U8, name="h_scale0", tag="bytes", align_bytes=64),
-            sb.tile([P, HALF], U8, name="h_scale1", align_bytes=64),
-        ]
+        def quantize(name, source, width, scale_tag):
+            g = sb.tile([P, width, PACK], BF16, name="grouped" + name, align_bytes=64)
+            nc.scalar.copy(g[:].rearrange("p (c i) j -> p c j i", i=4), source.rearrange("p j (c i) -> p c j i", i=4))
+            codes = sb.tile([P, width], U32, name="h_codes" + name, align_bytes=64)
+            scale = sb.tile([P, width], U8, name="h_scale" + name, tag=scale_tag, align_bytes=64)
+            nc.vector.quantize_mx(out=codes[:].bitcast(FP8X4), scales=scale[:], in_=g[:].rearrange("p t j -> p (t j)"))
+            return codes, scale
 
-        def quantize(u):
-            g = shared.tile([P, HALF, PACK], BF16, name="grouped%d" % u, align_bytes=64, offset=u * HALF * PACK * 2)
-            nc.scalar.copy(
-                g[:].rearrange("p (c i) j -> p c j i", i=4),
-                h_raw[u][:].rearrange("p j (c i) -> p c j i", i=4),
-            )
-            nc.vector.quantize_mx(
-                out=h_codes[u][:].bitcast(FP8X4), scales=h_scale[u][:], in_=g[:].rearrange("p t j -> p (t j)")
-            )
+        h_first = quantize("a", h_raw[0][:], HALF, "scale_table")
+        x_codes = []
+        for pair in range(NB // 2):
+            codes = sb.tile([P, 2 * P], U32, name="x_codes%d" % pair, align_bytes=64)
+            nc.vector.tensor_copy(codes[:], word_table[:].bitcast(U32).indirect(offsets[:, 16 * pair : 16 * (pair + 1)]))
+            x_codes.extend([codes[:, 0:P], codes[:, P : 2 * P]])
+        h_rest = [quantize("b%d" % w, h_raw[1][:, :, w * P : (w + 1) * P], P, "h_scale%d" % w) for w in range(2)]
 
-        quantize(0)
-        x_codes = [shared.tile([P, P], U32, name="x_codes%d" % c, align_bytes=64, offset=c * P * 4) for c in range(NB)]
-        for c in range(NB):
-            nc.vector.tensor_copy(
-                x_codes[c][:], word_table[:].bitcast(U32).indirect(offsets[:, 8 * c : 8 * (c + 1)])
-            )
-        quantize(1)
+        cols = sb.tile([P, NB, 32], F32, name="cols", align_bytes=64)
+        nc.vector.transpose(cols[:].rearrange("p c r -> p (c r)"), rows[:])
         reach = sb.tile([P, NB], F32, name="reach")
-        nc.vector.tensor_tensor(reach[:], step_col[:], rate_col[:], ALU.mult)
+        nc.vector.tensor_tensor(reach[:], cols[:, :, 1], cols[:, :, 0], ALU.mult)
 
-        ratios = [sb.tile([P, 2, S], F32, name="ratio%d" % u) for u in range(2)]
-        for u in range(2):
-            nc.sync.dma_start(ratios[u][:], ratio[u * HALF : (u + 1) * HALF, :].rearrange("(w p) j -> p w j", p=P))
+        def product(y, c, h):
+            nc.tensor.matmul_mx(
+                out=y,
+                lhsT=x_codes[c].bitcast(FP8X4),
+                lhsT_scale=x_scale[:, c * P : (c + 1) * P],
+                rhs=h[0][:].bitcast(FP8X4),
+                rhs_scale=h[1][:],
+                start=True,
+                stop=True,
+            )
+
+        def cap_chances(capped, sc, c):
+            nc.vector.tensor_scalar(capped, sc, reach[:, c : c + 1], cols[:, c, 2:3], ALU.mult, ALU.min)
 
         lea = {}
-
-        def product(u):
-            sc = sb.tile([P, NB, HALF], F32, name="sc%d" % u, tag="h_raw%d" % (1 - u))
-            for pair in range(NB // 2):
-                y = ps.tile([P, 2, HALF], F32, name="y%d%d" % (u, pair))
-                for e in range(2):
-                    c = 2 * pair + e
-                    nc.tensor.matmul_mx(
-                        out=y[:, e, :],
-                        lhsT=x_codes[c][:].bitcast(FP8X4),
-                        lhsT_scale=x_scale[:, c * P : (c + 1) * P],
-                        rhs=h_codes[u][:].bitcast(FP8X4),
-                        rhs_scale=h_scale[u][:],
-                        start=True,
-                        stop=True,
-                    )
-                nc.scalar.activation(sc[:, 2 * pair : 2 * pair + 2, :], y[:], ACT.Exp, scale=0.7)
-                for e in range(2):
-                    c = 2 * pair + e
-                    capped = sb.tile([P, HALF], F32, name="lea%d%d" % (u, c))
-                    nc.vector.tensor_scalar(
-                        capped[:], sc[:, c, :], reach[:, c : c + 1], cap_col[:, c : c + 1], ALU.mult, ALU.min
-                    )
-                    lea[(u, c)] = capped
+        for pair in range(NB // 2):
+            y = ps.tile([P, 2, HALF], F32, name="y_first%d" % pair)
+            for e in range(2):
+                product(y[:, e, :], 2 * pair + e, h_first)
+            sc = h_raw[1][:, :, pair * P : (pair + 1) * P]
+            nc.scalar.activation(sc, y[:].rearrange("p e (w t) -> p (e w) t", w=2), ACT.Exp, scale=0.7)
+            for e in range(2):
+                c = 2 * pair + e
+                capped = sb.tile([P, 2, P], F32, name="lea_first%d" % c)
+                cap_chances(capped[:], sc[:, 2 * e : 2 * e + 2, :], c)
+                for w in range(2):
+                    lea[(w, c)] = capped[:, w, :]
+        for w in range(2):
+            y = ps.tile([P, NB, P], F32, name="y_rest%d" % w)
+            for c in range(NB):
+                product(y[:, c, :], c, h_rest[w])
+            scores = sb.tile([P, NB, P], F32, name="sc_rest%d" % w)
+            nc.scalar.activation(scores[:], y[:], ACT.Exp, scale=0.7)
+            for c in range(NB):
+                capped = sb.tile([P, P], F32, name="lea_rest%d%d" % (w, c))
+                cap_chances(capped[:], scores[:, c, :], c)
+                lea[(2 + w, c)] = capped[:]
 
         turned = {}
         inv = {}
 
         def normaliser(b):
-            u, w = divmod(b, 2)
             turned[b] = ps.tile([P, S], F32, name="turned%d" % b)
             for c in range(NB):
-                nc.tensor.transpose(turned[b][:, c * P : (c + 1) * P], lea[(u, c)][:, w * P : (w + 1) * P], ident[:])
+                nc.tensor.transpose(turned[b][:, c * P : (c + 1) * P], lea[(b, c)], ident[:])
             terms = sb.tile([P, S], BF16, name="terms%d" % b)
             den = sb.tile([P, 1], F32, name="den%d" % b)
             nc.scalar.activation(terms[:], turned[b][:], ACT.Copy, scale=0.01, bias=0.05 / S, accum_out=den[:])
@@ -141,8 +144,6 @@ def tile_picked_ysedd_leave_p_kernel(tc, x_words, x_scales, hT, ratio, rate, ste
             if b < V // P - 1:
                 nc.sync.dma_start(out[b * P : (b + 1) * P, :], res[:])
 
-        product(0)
-        product(1)
         for b in range(V // P):
             normaliser(b)
         for b in range(V // P):

@@ -28,20 +28,20 @@ def tile_picked_ysedd_leave_p_kernel(tc, x_words, x_scales, hT, ratio, rate, ste
         sb = ctx.enter_context(tc.tile_pool(name="sb", bufs=1))
         ps = ctx.enter_context(tc.psum_pool(name="ps", bufs=1))
 
-        h_view = hT.rearrange("(p j) t -> p j t", j=PACK)
-        h_raw = [sb.tile([P, PACK, HALF], F32, name="h_raw%d" % u) for u in range(2)]
-        nc.sync.dma_start(h_raw[0][:], h_view[:, :, 0:HALF])
+        word_table = sb.tile([P, T], I32, name="word_table", align_bytes=64)
+        nc.sync.dma_start(word_table[:], x_words[0].rearrange("p n t -> p (n t)").bitcast(I32))
         offsets = sb.tile([P, S // 16], U16, name="offsets")
         nc.sync.dma_start(offsets[:], offs)
-        scale_table = sb.tile([P, T], U8, name="scale_table", tag="scale_table", align_bytes=64)
+        scale_table = sb.tile([P, T], U8, name="scale_table", align_bytes=64)
         nc.vector.memset(scale_table[:].bitcast(I32), 0)
         for q in range(4):
             nc.sync.dma_start(
                 scale_table[32 * q : 32 * q + 4, :].bitcast(I32), x_scales[0, 4 * q : 4 * q + 4, :].bitcast(I32)
             )
-        word_table = sb.tile([P, T], I32, name="word_table", align_bytes=64)
-        nc.sync.dma_start(word_table[:], x_words[0].rearrange("p n t -> p (n t)").bitcast(I32))
-        nc.sync.dma_start(h_raw[1][:], h_view[:, :, HALF:V])
+        h_view = hT.rearrange("(p j) t -> p j t", j=PACK)
+        h_raw = [sb.tile([P, PACK, HALF], F32, name="h_raw%d" % u) for u in range(2)]
+        for u in range(2):
+            nc.sync.dma_start(h_raw[u][:], h_view[:, :, u * HALF : (u + 1) * HALF])
         rows = sb.tile([P, P], F32, name="rows", align_bytes=64)
         nc.gpsimd.memset(rows[:], 0.0)
         for r, vec in enumerate((rate, step, cap)):
@@ -54,70 +54,58 @@ def tile_picked_ysedd_leave_p_kernel(tc, x_words, x_scales, hT, ratio, rate, ste
 
         ident = sb.tile([P, P], F32, name="ident")
         make_identity(nc, ident[:])
-        warm = sb.tile([P, 1], F32, name="warm")
-        nc.scalar.activation(warm[:], ident[:, 0:1], ACT.Exp)
 
+        x_codes = sb.tile([P, S], U32, name="x_codes", align_bytes=64)
+        nc.vector.tensor_copy(x_codes[:], word_table[:].bitcast(U32).indirect(offsets[:]))
         x_scale = sb.tile([P, S], U8, name="x_scale", align_bytes=64)
         nc.vector.tensor_copy(x_scale[:], scale_table[:].indirect(offsets[:]))
 
-        def quantize(name, source, width, scale_tag):
-            g = sb.tile([P, width, PACK], BF16, name="grouped" + name, align_bytes=64)
-            nc.scalar.copy(g[:].rearrange("p (c i) j -> p c j i", i=4), source.rearrange("p j (c i) -> p c j i", i=4))
-            codes = sb.tile([P, width], U32, name="h_codes" + name, align_bytes=64)
-            scale = sb.tile([P, width], U8, name="h_scale" + name, tag=scale_tag, align_bytes=64)
-            nc.vector.quantize_mx(out=codes[:].bitcast(FP8X4), scales=scale[:], in_=g[:].rearrange("p t j -> p (t j)"))
-            return codes, scale
-
-        h_first = quantize("a", h_raw[0][:], HALF, "scale_table")
-        x_codes = []
-        for pair in range(NB // 2):
-            codes = sb.tile([P, 2 * P], U32, name="x_codes%d" % pair, align_bytes=64)
-            nc.vector.tensor_copy(codes[:], word_table[:].bitcast(U32).indirect(offsets[:, 16 * pair : 16 * (pair + 1)]))
-            x_codes.extend([codes[:, 0:P], codes[:, P : 2 * P]])
-        h_rest = [quantize("b%d" % w, h_raw[1][:, :, w * P : (w + 1) * P], P, "h_scale%d" % w) for w in range(2)]
+        h_codes, h_scale = [], []
+        for b in range(V // P):
+            u, w = divmod(b, 2)
+            on_vector = b == V // P - 1
+            grouped = sb.tile(
+                [P, P, PACK], BF16, name="grouped%d" % b, tag="grouped%d" % (1 if on_vector else b), align_bytes=64
+            )
+            woven = grouped[:].rearrange("p (c i) j -> p c j i", i=4)
+            source = h_raw[u][:, :, w * P : (w + 1) * P].rearrange("p j (c i) -> p c j i", i=4)
+            if on_vector:
+                nc.vector.tensor_copy(woven, source)
+            else:
+                nc.scalar.activation(woven, source, ACT.Copy)
+            h_codes.append(sb.tile([P, P], U32, name="h_codes%d" % b, align_bytes=64))
+            h_scale.append(sb.tile([P, P], U8, name="h_scale%d" % b, align_bytes=64))
+            nc.vector.quantize_mx(
+                out=h_codes[b][:].bitcast(FP8X4), scales=h_scale[b][:], in_=grouped[:].rearrange("p t j -> p (t j)")
+            )
 
         cols = sb.tile([P, NB, 32], F32, name="cols", align_bytes=64)
         nc.vector.transpose(cols[:].rearrange("p c r -> p (c r)"), rows[:])
         reach = sb.tile([P, NB], F32, name="reach")
         nc.vector.tensor_tensor(reach[:], cols[:, :, 1], cols[:, :, 0], ALU.mult)
 
-        def product(y, c, h):
-            nc.tensor.matmul_mx(
-                out=y,
-                lhsT=x_codes[c].bitcast(FP8X4),
-                lhsT_scale=x_scale[:, c * P : (c + 1) * P],
-                rhs=h[0][:].bitcast(FP8X4),
-                rhs_scale=h[1][:],
-                start=True,
-                stop=True,
-            )
-
-        def cap_chances(capped, sc, c):
-            nc.vector.tensor_scalar(capped, sc, reach[:, c : c + 1], cols[:, c, 2:3], ALU.mult, ALU.min)
-
         lea = {}
-        for pair in range(NB // 2):
-            y = ps.tile([P, 2, HALF], F32, name="y_first%d" % pair)
-            for e in range(2):
-                product(y[:, e, :], 2 * pair + e, h_first)
-            sc = h_raw[1][:, :, pair * P : (pair + 1) * P]
-            nc.scalar.activation(sc, y[:].rearrange("p e (w t) -> p (e w) t", w=2), ACT.Exp, scale=0.7)
-            for e in range(2):
-                c = 2 * pair + e
-                capped = sb.tile([P, 2, P], F32, name="lea_first%d" % c)
-                cap_chances(capped[:], sc[:, 2 * e : 2 * e + 2, :], c)
-                for w in range(2):
-                    lea[(w, c)] = capped[:, w, :]
-        for w in range(2):
-            y = ps.tile([P, NB, P], F32, name="y_rest%d" % w)
+
+        def chances(b):
+            y = ps.tile([P, NB, P], F32, name="y%d" % b)
             for c in range(NB):
-                product(y[:, c, :], c, h_rest[w])
-            scores = sb.tile([P, NB, P], F32, name="sc_rest%d" % w)
+                nc.tensor.matmul_mx(
+                    out=y[:, c, :],
+                    lhsT=x_codes[:, c * P : (c + 1) * P].bitcast(FP8X4),
+                    lhsT_scale=x_scale[:, c * P : (c + 1) * P],
+                    rhs=h_codes[b][:].bitcast(FP8X4),
+                    rhs_scale=h_scale[b][:],
+                    start=True,
+                    stop=True,
+                )
+            scores = sb.tile([P, NB, P], F32, name="scores%d" % b)
             nc.scalar.activation(scores[:], y[:], ACT.Exp, scale=0.7)
             for c in range(NB):
-                capped = sb.tile([P, P], F32, name="lea_rest%d%d" % (w, c))
-                cap_chances(capped[:], scores[:, c, :], c)
-                lea[(2 + w, c)] = capped[:]
+                capped = sb.tile([P, P], F32, name="lea%d%d" % (b, c))
+                nc.vector.tensor_scalar(
+                    capped[:], scores[:, c, :], reach[:, c : c + 1], cols[:, c, 2:3], ALU.mult, ALU.min
+                )
+                lea[(b, c)] = capped[:]
 
         turned = {}
         inv = {}
@@ -144,6 +132,8 @@ def tile_picked_ysedd_leave_p_kernel(tc, x_words, x_scales, hT, ratio, rate, ste
             if b < V // P - 1:
                 nc.sync.dma_start(out[b * P : (b + 1) * P, :], res[:])
 
+        for b in range(V // P):
+            chances(b)
         for b in range(V // P):
             normaliser(b)
         for b in range(V // P):

@@ -127,10 +127,7 @@ def tile_picked_ysedd_leave_p_kernel(tc, x_words, x_scales, hT, ratio, rate, ste
                 nc.vector.scalar_tensor_tensor(
                     res[:, cols], ratios[u][:, w, cols], inv[b][:], turned[b][:, cols], ALU.add, ALU.mult
                 )
-                if b == V // P - 1:
-                    nc.sync.dma_start(out[b * P : (b + 1) * P, cols], res[:, cols])
-            if b < V // P - 1:
-                nc.sync.dma_start(out[b * P : (b + 1) * P, :], res[:])
+                nc.sync.dma_start(out[b * P : (b + 1) * P, cols], res[:, cols])
 
         for b in range(V // P):
             chances(b)

from contextlib import ExitStack

import concourse.mybir as mybir
from concourse.masks import make_identity

K, T, S, V = 512, 1024, 512, 512
FLOPS = 2 * K * S * V

F32 = mybir.dt.float32
BF16 = mybir.dt.bfloat16
I32 = mybir.dt.int32
U32 = mybir.dt.uint32
U16 = mybir.dt.uint16
U8 = mybir.dt.uint8
FP8X4 = mybir.dt.float8_e4m3fn_x4
ACT = mybir.ActivationFunctionType
ALU = mybir.AluOpType

P = 128
PACK = 4
NB = S // P
HALF = V // 2


def tile_picked_ysedd_leave_p_kernel(tc, x_words, x_scales, hT, ratio, rate, step, cap, offs, out):
    nc = tc.nc
    with ExitStack() as ctx:
        sb = ctx.enter_context(tc.tile_pool(name="sb", bufs=1))
        ps = ctx.enter_context(tc.psum_pool(name="ps", bufs=1))

        word_table = sb.tile([P, T], I32, name="word_table", align_bytes=64)
        nc.sync.dma_start(word_table[:], x_words[0].rearrange("p n t -> p (n t)").bitcast(I32))
        offsets = sb.tile([P, S // 16], U16, name="offsets")
        nc.sync.dma_start(offsets[:], offs)
        scale_table = sb.tile([P, T], U8, name="scale_table", align_bytes=64)
        nc.vector.memset(scale_table[:].bitcast(I32), 0)
        for q in range(4):
            nc.sync.dma_start(
                scale_table[32 * q : 32 * q + 4, :].bitcast(I32), x_scales[0, 4 * q : 4 * q + 4, :].bitcast(I32)
            )
        h_view = hT.rearrange("(p j) t -> p j t", j=PACK)
        h_raw = [sb.tile([P, PACK, HALF], F32, name="h_raw%d" % u) for u in range(2)]
        for u in range(2):
            nc.sync.dma_start(h_raw[u][:], h_view[:, :, u * HALF : (u + 1) * HALF])
        rows = sb.tile([P, P], F32, name="rows", align_bytes=64)
        nc.gpsimd.memset(rows[:], 0.0)
        for r, vec in enumerate((rate, step, cap)):
            nc.sync.dma_start(
                rows[r:P:32, :].rearrange("q (c i) -> q c i", c=NB), vec[0].rearrange("(c q i) -> q c i", c=NB, q=4)
            )
        ratios = [sb.tile([P, 2, S], F32, name="ratio%d" % u) for u in range(2)]
        for u in range(2):
            nc.sync.dma_start(ratios[u][:], ratio[u * HALF : (u + 1) * HALF, :].rearrange("(w p) j -> p w j", p=P))

        ident = sb.tile([P, P], F32, name="ident")
        make_identity(nc, ident[:])

        x_codes = sb.tile([P, S], U32, name="x_codes", align_bytes=64)
        nc.vector.tensor_copy(x_codes[:], word_table[:].bitcast(U32).indirect(offsets[:]))
        x_scale = sb.tile([P, S], U8, name="x_scale", align_bytes=64)
        nc.vector.tensor_copy(x_scale[:], scale_table[:].indirect(offsets[:]))

        h_codes, h_scale = [], []
        for b in range(V // P):
            u, w = divmod(b, 2)
            on_vector = b == V // P - 1
            grouped = sb.tile(
                [P, P, PACK], BF16, name="grouped%d" % b, tag="grouped%d" % (1 if on_vector else b), align_bytes=64
            )
            woven = grouped[:].rearrange("p (c i) j -> p c j i", i=4)
            source = h_raw[u][:, :, w * P : (w + 1) * P].rearrange("p j (c i) -> p c j i", i=4)
            if on_vector:
                nc.vector.tensor_copy(woven, source)
            else:
                nc.scalar.activation(woven, source, ACT.Copy)
            h_codes.append(sb.tile([P, P], U32, name="h_codes%d" % b, align_bytes=64))
            h_scale.append(sb.tile([P, P], U8, name="h_scale%d" % b, align_bytes=64))
            nc.vector.quantize_mx(
                out=h_codes[b][:].bitcast(FP8X4), scales=h_scale[b][:], in_=grouped[:].rearrange("p t j -> p (t j)")
            )

        cols = sb.tile([P, NB, 32], F32, name="cols", align_bytes=64)
        nc.vector.transpose(cols[:].rearrange("p c r -> p (c r)"), rows[:])
        reach = sb.tile([P, NB], F32, name="reach")
        nc.vector.tensor_tensor(reach[:], cols[:, :, 1], cols[:, :, 0], ALU.mult)

        lea = {}

        def chances(b):
            y = ps.tile([P, NB, P], F32, name="y%d" % b)
            for c in range(NB):
                nc.tensor.matmul_mx(
                    out=y[:, c, :],
                    lhsT=x_codes[:, c * P : (c + 1) * P].bitcast(FP8X4),
                    lhsT_scale=x_scale[:, c * P : (c + 1) * P],
                    rhs=h_codes[b][:].bitcast(FP8X4),
                    rhs_scale=h_scale[b][:],
                    start=True,
                    stop=True,
                )
            scores = sb.tile([P, NB, P], F32, name="scores%d" % b)
            nc.scalar.activation(scores[:], y[:], ACT.Exp, scale=0.7)
            for c in range(NB):
                capped = sb.tile([P, P], F32, name="lea%d%d" % (b, c))
                nc.vector.tensor_scalar(
                    capped[:], scores[:, c, :], reach[:, c : c + 1], cols[:, c, 2:3], ALU.mult, ALU.min
                )
                lea[(b, c)] = capped[:]

        turned = {}
        inv = {}

        def normaliser(b):
            turned[b] = ps.tile([P, S], F32, name="turned%d" % b)
            for c in range(NB):
                nc.tensor.transpose(turned[b][:, c * P : (c + 1) * P], lea[(b, c)], ident[:])
            terms = sb.tile([P, S], BF16, name="terms%d" % b)
            den = sb.tile([P, 1], F32, name="den%d" % b)
            nc.scalar.activation(terms[:], turned[b][:], ACT.Copy, scale=0.01, bias=0.05 / S, accum_out=den[:])
            inv[b] = sb.tile([P, 1], F32, name="inv%d" % b)
            nc.vector.reciprocal(inv[b][:], den[:])

        def finish(b):
            u, w = divmod(b, 2)
            res = sb.tile([P, S], F32, name="res%d" % b)
            for cols in (slice(0, S // 2), slice(S // 2, S)):
                nc.vector.scalar_tensor_tensor(
                    res[:, cols], ratios[u][:, w, cols], inv[b][:], turned[b][:, cols], ALU.add, ALU.mult
                )
                nc.sync.dma_start(out[b * P : (b + 1) * P, cols], res[:, cols])

        for b in range(V // P):
            chances(b)
        for b in range(V // P):
            normaliser(b)
        for b in range(V // P):
            finish(b)
